import numpy as np
import ml_dtypes


def mxq(x, axis, fmt="e4m3"):
    dtype, down = {"e4m3": (ml_dtypes.float8_e4m3fn, 7), "e5m2": (ml_dtypes.float8_e5m2, 14)}[fmt]
    v = np.moveaxis(np.asarray(x, np.float32).astype(ml_dtypes.bfloat16).astype(np.float64), axis, -1)
    blocks = v.reshape(v.shape[:-1] + (-1, 32))
    amax = np.abs(blocks).max(-1, keepdims=True)
    byte = np.maximum(np.where(amax > 0, np.frexp(amax)[1] - 1 + 127, 0) - down, 1)
    scale = np.exp2(byte - 127.0)
    codes = (blocks / scale).astype(np.float32).astype(dtype).astype(np.float64)
    return np.moveaxis((codes * scale).reshape(v.shape), -1, axis)


WIDE = False


def mx_kscale(k):
    if not WIDE:
        return np.ones(k)
    levels = np.array([10, -10, 5, -5, 0])
    if k % 512:
        return np.exp2(np.random.permutation(np.resize(levels, k // 32))).repeat(32)
    a = np.empty((k // 512, 16))
    for p in range(k // 512):
        a[p, :8] = np.random.permutation(np.resize(levels, 8))
        for g in range(8):
            far = levels[np.abs(levels - a[p, g]) >= 10]
            a[p, g + 8] = far[np.random.randint(len(far))]
    return np.exp2(a.ravel()).repeat(32)


def f64(x):
    return np.asarray(x).astype(np.float64)


def striped(idx):
    return np.tile(idx.reshape(-1, 16).T, (8, 1)).astype(np.uint16)


def unstriped(offs):
    return offs[:16].T.reshape(-1).astype(np.int64)


def striped8(idx):
    return np.concatenate([x.reshape(-1, 16).T for x in idx]).astype(np.uint16)


def runs(offs, k):
    lists = np.stack([offs[16 * r : 16 * r + 16].T.reshape(-1) for r in range(8)]).astype(np.int64)
    return lists[np.arange(k) % 512 // 64]


def pack_weight(w):
    k, n = w.shape
    w = f64(np.asarray(w, np.float32).astype(ml_dtypes.bfloat16)).reshape(k // 32, 32, n)
    amax = np.abs(w).max(1)
    byte = np.clip(np.where(amax > 0, np.frexp(amax)[1] - 1 + 127 - 7, 1), 1, 254)
    scaled = (w * np.exp2(127.0 - byte)[:, None, :]).reshape(k, n).astype(np.float32)
    words = np.ascontiguousarray(scaled.reshape(k // 512, 128, 4, n).transpose(0, 1, 3, 2)).astype(ml_dtypes.float8_e4m3fn).view(np.uint8)
    return words, np.ascontiguousarray(byte.astype(np.uint8).reshape(k // 512, 16, n))


def unpack_weight(words, scales):
    g, p, n, _ = words.shape
    vals = np.ascontiguousarray(words).view(ml_dtypes.float8_e4m3fn).astype(np.float64) * np.repeat(np.exp2(scales.astype(np.float64) - 127.0), 8, axis=1)[..., None]
    return vals.transpose(0, 1, 3, 2).reshape(g * 512, n)


E2M1 = np.array([0.0, 0.5, 1.0, 1.5, 2.0, 3.0, 4.0, 6.0, -0.0, -0.5, -1.0, -1.5, -2.0, -3.0, -4.0, -6.0])


def pack_fp4(w):
    k, n = w.shape
    w = f64(np.asarray(w, np.float32).astype(ml_dtypes.bfloat16)).reshape(k // 32, 32, n)
    amax = np.abs(w).max(1)
    mant, ex = np.frexp(amax / 6.0)
    byte = np.clip(np.where(amax > 0, np.where(mant > 0.5, ex, ex - 1) + 127, 1), 1, 254)
    scaled = (w * np.exp2(127.0 - byte)[:, None, :]).reshape(k, n).astype(np.float32)
    c = np.ascontiguousarray(scaled.reshape(k // 512, 128, 4, n).transpose(0, 1, 3, 2)).astype(ml_dtypes.float4_e2m1fn).view(np.uint8) & 0xF
    words = (c[..., 0::2] | (c[..., 1::2] << 4)).reshape(k // 512, 128, 2 * n)
    return np.ascontiguousarray(words), np.ascontiguousarray(byte.astype(np.uint8).reshape(k // 512, 16, n))


def unpack_fp4(words, scales):
    g, _, n = scales.shape
    words = np.ascontiguousarray(words).reshape(g, 128, n, 2)
    nib = np.empty((g, 128, n, 4), np.uint8)
    nib[..., 0::2] = words & 0xF
    nib[..., 1::2] = words >> 4
    vals = E2M1[nib] * np.repeat(np.exp2(scales.astype(np.float64) - 127.0), 8, axis=1)[..., None]
    return vals.transpose(0, 1, 3, 2).reshape(g * 512, n)


def planes(y):
    n, m = y.shape
    v = y.astype(np.float32).astype(ml_dtypes.bfloat16).astype(np.float64).reshape(n // 32, 32, m)
    top = np.abs(v).max(1)
    byte = np.clip(np.where(top > 0, np.frexp(top)[1] - 1 + 127 - 7, 1), 1, 254)
    codes = (v * np.exp2(127.0 - byte)[:, None, :]).reshape(n, m).astype(np.float32).astype(ml_dtypes.float8_e4m3fn).view(np.uint8)
    words = codes.reshape(n // 512, 128, 4, m).transpose(0, 1, 3, 2)
    return np.ascontiguousarray(words), np.ascontiguousarray(byte.astype(np.uint8).reshape(n // 512, 16, m))


K, T, S, N, H = 512, 2048, 512, 512, 512


def setup_inputs():
    n = np.random.standard_normal
    s = mx_kscale(K)[:, None]
    u = mx_kscale(H)
    packed_xT = pack_weight(n((K, T)) * s)
    packed_w1 = pack_fp4(n((K, H)) / np.sqrt(K) / s)
    packed_w2 = pack_fp4(n((H, H)) / np.sqrt(H) / u[:, None])
    packed_w3 = pack_fp4(n((H, N)) / np.sqrt(H) / u[:, None])
    return {
        "x_words": packed_xT[0],
        "x_scales": packed_xT[1],
        "w1_words": packed_w1[0],
        "w1_scales": packed_w1[1],
        "gn": (np.random.uniform(0.5, 1.5, (H, 1)) * u[:, None]).astype(np.float32),
        "w2_words": packed_w2[0],
        "w2_scales": packed_w2[1],
        "res": n((N, S)).astype(np.float32),
        "w3_words": packed_w3[0],
        "w3_scales": packed_w3[1],
        "offs": striped(np.random.permutation(T)[:S]),
        "d1": striped8(np.stack([np.random.permutation(S) for _ in range(8)])),
        "d2": striped8(np.stack([np.random.permutation(S) for _ in range(8)])),
        "mv": striped8(np.stack([np.random.permutation(S) for _ in range(8)])),
    }


def reference(x_words, x_scales, w1_words, w1_scales, gn, w2_words, w2_scales, res, w3_words, w3_scales, offs, d1, d2, mv):
    xq = unpack_weight(x_words, x_scales)[:, unstriped(offs)]
    y = unpack_fp4(w1_words, w1_scales).T @ xq
    v1 = y - (0.5 * (y[np.arange(H)[:, None], runs(d1, H)]))
    w = 0.5 * v1 + v1[np.arange(H)[:, None], runs(d1, H)]
    u1 = w - (0.25 * (w[np.arange(H)[:, None], runs(d2, H)]))
    z = f64(gn) * (0.25 * u1 + u1[np.arange(H)[:, None], runs(d2, H)])
    h = np.tanh(unpack_fp4(w2_words, w2_scales).T @ mxq(z, 0, "e4m3"))
    z2 = f64(gn) * (h[np.arange(H)[:, None], runs(mv, H)])
    out_0 = f64(res) + (unpack_fp4(w3_words, w3_scales).T @ mxq(z2, 0, "e4m3"))
    return (out_0,) + planes(out_0)

@@ -1,0 +1,228 @@
+from contextlib import ExitStack
+
+import concourse.mybir as mybir
+
+F32 = mybir.dt.float32
+BF16 = mybir.dt.bfloat16
+I32 = mybir.dt.int32
+U32 = mybir.dt.uint32
+U16 = mybir.dt.uint16
+U8 = mybir.dt.uint8
+FP8X4 = mybir.dt.float8_e4m3fn_x4
+FP4X4 = mybir.dt.float4_e2m1fn_x4
+ADD = mybir.AluOpType.add
+MULT = mybir.AluOpType.mult
+COPY = mybir.ActivationFunctionType.Copy
+TANH = mybir.ActivationFunctionType.Tanh
+
+P = 128
+PACK = 4
+T = 2048
+S = 512
+HALF = 256
+CHUNK = 128
+N_CHUNKS = S // CHUNK
+FLOPS = 3 * 2 * 512 * 512 * 512
+
+
+def tile_picked_allpass2_none_po_kernel(tc, x_words, x_scales, w1_words, w1_scales, gn, w2_words, w2_scales, res, w3_words, w3_scales, offs, d1, d2, mv, out_0, out_1, out_2):
+    nc = tc.nc
+    with ExitStack() as ctx:
+        lists = ctx.enter_context(tc.tile_pool(name="lists", bufs=1))
+        keep = ctx.enter_context(tc.tile_pool(name="keep", bufs=1))
+        psum = ctx.enter_context(tc.psum_pool(name="psum", bufs=8))
+
+        def load_list(src, name):
+            tile = lists.tile([P, S // 16], U16, name=name)
+            nc.sync.dma_start(tile[:], src)
+            return tile
+
+        def entries(tile, start, count):
+            return tile[:, start // 16 : (start + count) // 16]
+
+        def load_scale_rows(queue, tile, src):
+            for q in range(4):
+                queue.dma_start(tile[32 * q : 32 * q + 4, :].bitcast(I32), src[0, 4 * q : 4 * q + 4, :].bitcast(I32))
+
+        def load_words(queue, src, name):
+            raw = keep.tile([P, 2 * S], U8, name=name, align_bytes=64)
+            queue.dma_start(raw[:].bitcast(I32), src[0].bitcast(I32))
+            return raw
+
+        def deal_words(raw, name, tag):
+            dealt = keep.tile([P, 2 * S], U8, name=name, tag=tag, align_bytes=64)
+            nc.vector.tensor_copy(
+                dealt[:].rearrange("p (t m b) -> p t m b", t=PACK, b=2),
+                raw[:].rearrange("p (m t b) -> p t m b", t=PACK, b=2),
+            )
+            return dealt
+
+        def deal_scales(raw, name, tag):
+            dealt = keep.tile([P, S], U8, name=name, tag=tag, align_bytes=64)
+            nc.vector.tensor_copy(
+                dealt[:].rearrange("p (t m) -> p t m", t=PACK),
+                raw[:].rearrange("p (m t) -> p t m", t=PACK),
+            )
+            return dealt
+
+        def zeroed_scales(name, width):
+            raw = keep.tile([P, width], U8, name=name, align_bytes=64)
+            nc.gpsimd.memset(raw[:].bitcast(I32), 0)
+            return raw
+
+        def product(dst, words, scales, t, codes, code_scales):
+            nc.tensor.matmul_mx(
+                out=dst,
+                lhsT=words[:, 2 * P * t : 2 * P * (t + 1)].bitcast(FP4X4),
+                lhsT_scale=scales[:, P * t : P * (t + 1)],
+                rhs=codes.bitcast(FP8X4),
+                rhs_scale=code_scales,
+                start=True,
+                stop=True,
+            )
+
+        def rows(name):
+            return [keep.tile([P, S], F32, name="%s_rows%d" % (name, t)) for t in range(PACK)]
+
+        def weave(copy, src, name, tag):
+            woven = keep.tile([P, CHUNK, PACK], BF16, name=name, tag=tag, align_bytes=64)
+            copy(
+                woven[:].rearrange("p (c i) t -> p c t i", i=4),
+                src[:].rearrange("p t (c i) -> p c t i", i=4),
+            )
+            return woven
+
+        def quantize(woven, codes, scales):
+            nc.vector.quantize_mx(out=codes.bitcast(FP8X4), scales=scales, in_=woven[:].rearrange("p c t -> p (c t)"))
+
+        xs_raw = zeroed_scales("xs_raw", T)
+        w1s_raw = zeroed_scales("w1s_raw", S)
+        w2s_raw = zeroed_scales("w2s_raw", S)
+        w3s_raw = zeroed_scales("w3s_raw", S)
+        load_scale_rows(nc.sync, xs_raw, x_scales)
+        w1_raw = load_words(nc.scalar, w1_words, "w1_raw")
+        gn_sb = keep.tile([P, PACK], F32, name="gn_sb")
+        nc.scalar.dma_start(gn_sb[:], gn.rearrange("(p t) o -> p (t o)", t=PACK))
+        xw_raw = keep.tile([P, T], I32, name="xw_raw", tag="big", align_bytes=64)
+        nc.scalar.dma_start(xw_raw[:], x_words[0].rearrange("p n t -> p (n t)").bitcast(I32))
+        offs_sb = load_list(offs, "offs_sb")
+        load_scale_rows(nc.sync, w1s_raw, w1_scales)
+        d1_sb = load_list(d1, "d1_sb")
+        w2_raw = load_words(nc.sync, w2_words, "w2_raw")
+        load_scale_rows(nc.sync, w2s_raw, w2_scales)
+        d2_sb = load_list(d2, "d2_sb")
+        mv_sb = load_list(mv, "mv_sb")
+        w3_raw = load_words(nc.sync, w3_words, "w3_raw")
+        load_scale_rows(nc.sync, w3s_raw, w3_scales)
+
+        warm = keep.tile([P, 1], F32, name="warm")
+        nc.scalar.activation(warm[:], gn_sb[:, 0:1], TANH)
+        gain = keep.tile([P, PACK], F32, name="gain")
+        nc.scalar.activation(gain[:], gn_sb[:], COPY, scale=0.125)
+        gain_m2 = keep.tile([P, PACK], F32, name="gain_m2")
+        nc.scalar.activation(gain_m2[:], gn_sb[:], COPY, scale=-0.25)
+
+        w1 = deal_words(w1_raw, "w1", "w1")
+        xs = keep.tile([P, S], U8, name="xs", align_bytes=64)
+        nc.vector.tensor_copy(xs[:], xs_raw[:].indirect(offs_sb[:]))
+        w1s = deal_scales(w1s_raw, "w1s", "w1s")
+
+        y, y_m2 = rows("y"), rows("y_m2")
+        banks = {}
+        for h in range(2):
+            xw = keep.tile([P, HALF], U32, name="xw%d" % h, align_bytes=64)
+            nc.vector.tensor_copy(xw[:], xw_raw[:].bitcast(U32).indirect(entries(offs_sb, h * HALF, HALF)))
+            for t in range(PACK):
+                banks[t, h] = psum.tile([P, S], F32, name="bank_y%d%d" % (t, h), tag="bank")
+                product(banks[t, h][:, :HALF], w1, w1s, t, xw[:], xs[:, h * HALF : (h + 1) * HALF])
+        for t in range(PACK):
+            for dst, scale in ((y, gain), (y_m2, gain_m2)):
+                for h in range(2):
+                    nc.scalar.activation(dst[t][:, h * HALF : (h + 1) * HALF], banks[t, h][:, :HALF], COPY, scale=scale[:, t : t + 1])
+
+        res_sb = keep.tile([P, PACK, S], F32, name="res_sb", tag="big", align_bytes=64)
+        nc.sync.dma_start(res_sb[:], res.rearrange("(p t) j -> p t j", t=PACK))
+        w2 = deal_words(w2_raw, "w2", "w2")
+        w2s = deal_scales(w2s_raw, "w2s", "w2s")
+
+        def stage(window, plain, lst, name, factor):
+            dst, scaled = rows(name), rows(name + "_s")
+            for t in range(PACK):
+                for h in range(2):
+                    cols = slice(h * HALF, (h + 1) * HALF)
+                    nc.vector.tensor_tensor(dst[t][:, cols], window[t][:].indirect(entries(lst, h * HALF, HALF)), plain[t][:, cols], ADD)
+                nc.scalar.activation(scaled[t][:], dst[t][:], COPY, scale=factor)
+            return dst, scaled
+
+        v, v_s = stage(y, y_m2, d1_sb, "v", 0.5)
+        w, w_s = stage(v, v_s, d1_sb, "w", -4.0)
+        u, u_s = stage(w, w_s, d2_sb, "u", 0.25)
+
+        gain_rows = keep.tile([P, PACK, CHUNK], F32, name="gain_rows")
+        nc.scalar.copy(gain_rows[:], gn_sb[:].unsqueeze(2).to_broadcast([P, PACK, CHUNK]))
+
+        hid = rows("hid")
+
+        def fetch(window, lst, plain, op, c, name, tag):
+            dst = keep.tile([P, PACK, CHUNK], F32, name=name, tag=tag)
+            for t in range(PACK):
+                nc.vector.tensor_tensor(dst[:, t, :], window[t][:].indirect(entries(lst, c * CHUNK, CHUNK)), plain(t), op)
+            return dst
+
+        def chunk_product(woven, words, scales, name):
+            codes = keep.tile([P, CHUNK], U32, name=name + "_codes", align_bytes=64)
+            code_scales = keep.tile([P, CHUNK], U8, name=name + "_scales", align_bytes=64)
+            quantize(woven, codes[:], code_scales[:])
+            bank = psum.tile([P, S], F32, name=name + "_bank", tag="bank")
+            for t in range(PACK):
+                product(bank[:, t * CHUNK : (t + 1) * CHUNK], words, scales, t, codes[:], code_scales[:])
+            return bank
+
+        def hidden(woven, c):
+            bank = chunk_product(woven, w2, w2s, "z%d" % c)
+            for t in range(PACK):
+                nc.scalar.activation(hid[t][:, c * CHUNK : (c + 1) * CHUNK], bank[:, t * CHUNK : (t + 1) * CHUNK], TANH)
+
+        woven_z = {}
+        for c in range(N_CHUNKS):
+            cols = slice(c * CHUNK, (c + 1) * CHUNK)
+            z = fetch(u, d2_sb, lambda t: u_s[t][:, cols], ADD, c, "z%d" % c, "z%d" % c)
+            copy = nc.vector.tensor_copy if c == N_CHUNKS - 1 else nc.scalar.copy
+            woven_z[c] = weave(copy, z, "zb%d" % c, "zb%d" % c)
+            if c > 0:
+                hidden(woven_z[c - 1], c - 1)
+        hidden(woven_z[N_CHUNKS - 1], N_CHUNKS - 1)
+        w3 = deal_words(w3_raw, "w3", "zb%d" % (N_CHUNKS - 1))
+        w3s = deal_scales(w3s_raw, "w3s", "zb%d" % (N_CHUNKS - 2))
+
+        out_rows = out_0.rearrange("(p t) j -> p t j", t=PACK)
+        out_words = out_1[0].rearrange("p n t -> p (n t)").bitcast(I32)
+        out_scales = keep.tile([P, S], U8, name="out_scales", align_bytes=64)
+        woven_z2, banks3, woven_out = {}, {}, {}
+
+        def finish(c):
+            cols = slice(c * CHUNK, (c + 1) * CHUNK)
+            result = keep.tile([P, PACK, CHUNK], F32, name="result%d" % c)
+            nc.vector.tensor_tensor(result[:], banks3[c][:].rearrange("p (t n) -> p t n", t=PACK), res_sb[:, :, cols], ADD)
+            nc.sync.dma_start(out_rows[:, :, cols], result[:])
+            woven_out[c] = weave(nc.scalar.copy, result, "ob%d" % c, "ob%d" % c)
+
+        def planes(c):
+            cols = slice(c * CHUNK, (c + 1) * CHUNK)
+            codes = keep.tile([P, CHUNK], U32, name="out_codes%d" % c, align_bytes=64)
+            quantize(woven_out[c], codes[:], out_scales[:, cols])
+            nc.sync.dma_start(out_words[:, cols], codes[:].bitcast(I32))
+
+        for step in range(N_CHUNKS + 3):
+            if step < N_CHUNKS:
+                z2 = fetch(hid, mv_sb, lambda t: gain_rows[:, t, :], MULT, step, "z2_%d" % step, "z2_%d" % step)
+                woven_z2[step] = weave(nc.scalar.copy, z2, "z2b%d" % step, "z2b%d" % step)
+            if 0 <= step - 1 < N_CHUNKS:
+                banks3[step - 1] = chunk_product(woven_z2[step - 1], w3, w3s, "z2q%d" % (step - 1))
+            if 0 <= step - 2 < N_CHUNKS:
+                finish(step - 2)
+            if 0 <= step - 3 < N_CHUNKS:
+                planes(step - 3)
+        for q in range(4):
+            queue = nc.sync if q % 2 == 0 else nc.scalar
+            queue.dma_start(out_2[0, 4 * q : 4 * q + 4, :].bitcast(I32), out_scales[32 * q : 32 * q + 4, :].bitcast(I32))

@@ -13,6 +13,8 @@ FP4X4 = mybir.dt.float4_e2m1fn_x4
 ADD = mybir.AluOpType.add
 MULT = mybir.AluOpType.mult
 COPY = mybir.ActivationFunctionType.Copy
+IDENTITY = mybir.ActivationFunctionType.Identity
+SIGMOID = mybir.ActivationFunctionType.Sigmoid
 TANH = mybir.ActivationFunctionType.Tanh
 
 P = 128
@@ -20,8 +22,9 @@ PACK = 4
 T = 2048
 S = 512
 HALF = 256
-CHUNK = 128
-N_CHUNKS = S // CHUNK
+Z_CHUNKS = [128, 128, 128, 128]
+OUT_CHUNKS = [128, 128, 128, 128]
+SCALAR_TILES = 1
 FLOPS = 3 * 2 * 512 * 512 * 512
 
 
@@ -37,23 +40,23 @@ def tile_picked_allpass2_none_po_kernel(tc, x_words, x_scales, w1_words, w1_scal
             nc.sync.dma_start(tile[:], src)
             return tile
 
-        def entries(tile, start, count):
-            return tile[:, start // 16 : (start + count) // 16]
+        def entries(tile, cols):
+            return tile[:, cols.start // 16 : cols.stop // 16]
 
-        def load_scale_rows(queue, tile, src):
-            for q in range(4):
+        def load_scale_rows(queue, tile, src, quadrants):
+            for q in quadrants:
                 queue.dma_start(tile[32 * q : 32 * q + 4, :].bitcast(I32), src[0, 4 * q : 4 * q + 4, :].bitcast(I32))
 
         def load_words(queue, src, name):
-            raw = keep.tile([P, 2 * S], U8, name=name, align_bytes=64)
+            raw = keep.tile([P, 2 * S], U8, name=name, tag="w_raw", align_bytes=64)
             queue.dma_start(raw[:].bitcast(I32), src[0].bitcast(I32))
             return raw
 
         def deal_words(raw, name, tag):
             dealt = keep.tile([P, 2 * S], U8, name=name, tag=tag, align_bytes=64)
             nc.vector.tensor_copy(
-                dealt[:].rearrange("p (t m b) -> p t m b", t=PACK, b=2),
-                raw[:].rearrange("p (m t b) -> p t m b", t=PACK, b=2),
+                dealt[:].bitcast(U16).rearrange("p (t m) -> p t m", t=PACK),
+                raw[:].bitcast(U16).rearrange("p (m t) -> p t m", t=PACK),
             )
             return dealt
 
@@ -81,11 +84,11 @@ def tile_picked_allpass2_none_po_kernel(tc, x_words, x_scales, w1_words, w1_scal
                 stop=True,
             )
 
-        def rows(name):
-            return [keep.tile([P, S], F32, name="%s_rows%d" % (name, t)) for t in range(PACK)]
+        def rows(name, width):
+            return [keep.tile([P, width], F32, name="%s_rows%d" % (name, t)) for t in range(PACK)]
 
-        def weave(copy, src, name, tag):
-            woven = keep.tile([P, CHUNK, PACK], BF16, name=name, tag=tag, align_bytes=64)
+        def weave(copy, src, name):
+            woven = keep.tile([P, src.shape[2], PACK], BF16, name=name, align_bytes=64)
             copy(
                 woven[:].rearrange("p (c i) t -> p c t i", i=4),
                 src[:].rearrange("p t (c i) -> p c t i", i=4),
@@ -95,133 +98,168 @@ def tile_picked_allpass2_none_po_kernel(tc, x_words, x_scales, w1_words, w1_scal
         def quantize(woven, codes, scales):
             nc.vector.quantize_mx(out=codes.bitcast(FP8X4), scales=scales, in_=woven[:].rearrange("p c t -> p (c t)"))
 
-        xs_raw = zeroed_scales("xs_raw", T)
+        def chunks(widths):
+            return [slice(sum(widths[:c]), sum(widths[: c + 1])) for c in range(len(widths))]
+
+        halves = chunks([HALF, HALF])
+
+        xs_raw = keep.tile([P, T], U8, name="xs_raw", tag="x_small", align_bytes=64)
+        nc.vector.memset(xs_raw[:, : T // 2].bitcast(I32), 0)
+        nc.gpsimd.memset(xs_raw[:, T // 2 :].bitcast(I32), 0)
         w1s_raw = zeroed_scales("w1s_raw", S)
-        w2s_raw = zeroed_scales("w2s_raw", S)
-        w3s_raw = zeroed_scales("w3s_raw", S)
-        load_scale_rows(nc.sync, xs_raw, x_scales)
-        w1_raw = load_words(nc.scalar, w1_words, "w1_raw")
+        w1_raw = load_words(nc.sync, w1_words, "w1_raw")
+        load_scale_rows(nc.sync, xs_raw, x_scales, range(4))
         gn_sb = keep.tile([P, PACK], F32, name="gn_sb")
         nc.scalar.dma_start(gn_sb[:], gn.rearrange("(p t) o -> p (t o)", t=PACK))
         xw_raw = keep.tile([P, T], I32, name="xw_raw", tag="big", align_bytes=64)
         nc.scalar.dma_start(xw_raw[:], x_words[0].rearrange("p n t -> p (n t)").bitcast(I32))
         offs_sb = load_list(offs, "offs_sb")
-        load_scale_rows(nc.sync, w1s_raw, w1_scales)
+        load_scale_rows(nc.sync, w1s_raw, w1_scales, (0, 1))
+        load_scale_rows(nc.gpsimd, w1s_raw, w1_scales, (2, 3))
         d1_sb = load_list(d1, "d1_sb")
-        w2_raw = load_words(nc.sync, w2_words, "w2_raw")
-        load_scale_rows(nc.sync, w2s_raw, w2_scales)
         d2_sb = load_list(d2, "d2_sb")
         mv_sb = load_list(mv, "mv_sb")
-        w3_raw = load_words(nc.sync, w3_words, "w3_raw")
-        load_scale_rows(nc.sync, w3s_raw, w3_scales)
+        w2s_raw = zeroed_scales("w2s_raw", S)
+        w3s_raw = zeroed_scales("w3s_raw", S)
 
         warm = keep.tile([P, 1], F32, name="warm")
-        nc.scalar.activation(warm[:], gn_sb[:, 0:1], TANH)
+        nc.scalar.activation(warm[:], gn_sb[:, 0:1], SIGMOID)
         gain = keep.tile([P, PACK], F32, name="gain")
         nc.scalar.activation(gain[:], gn_sb[:], COPY, scale=0.125)
         gain_m2 = keep.tile([P, PACK], F32, name="gain_m2")
         nc.scalar.activation(gain_m2[:], gn_sb[:], COPY, scale=-0.25)
+        gn_twice = keep.tile([P, PACK], F32, name="gn_twice")
+        nc.scalar.activation(gn_twice[:], gn_sb[:], COPY, scale=2.0)
+        gn_minus = keep.tile([P, PACK], F32, name="gn_minus")
+        nc.scalar.activation(gn_minus[:], gn_sb[:], COPY, scale=-1.0)
 
         w1 = deal_words(w1_raw, "w1", "w1")
+        w2_raw = load_words(nc.sync, w2_words, "w2_raw")
+        load_scale_rows(nc.sync, w2s_raw, w2_scales, range(4))
         xs = keep.tile([P, S], U8, name="xs", align_bytes=64)
         nc.vector.tensor_copy(xs[:], xs_raw[:].indirect(offs_sb[:]))
         w1s = deal_scales(w1s_raw, "w1s", "w1s")
 
-        y, y_m2 = rows("y"), rows("y_m2")
-        banks = {}
-        for h in range(2):
-            xw = keep.tile([P, HALF], U32, name="xw%d" % h, align_bytes=64)
-            nc.vector.tensor_copy(xw[:], xw_raw[:].bitcast(U32).indirect(entries(offs_sb, h * HALF, HALF)))
-            for t in range(PACK):
-                banks[t, h] = psum.tile([P, S], F32, name="bank_y%d%d" % (t, h), tag="bank")
-                product(banks[t, h][:, :HALF], w1, w1s, t, xw[:], xs[:, h * HALF : (h + 1) * HALF])
-        for t in range(PACK):
-            for dst, scale in ((y, gain), (y_m2, gain_m2)):
-                for h in range(2):
-                    nc.scalar.activation(dst[t][:, h * HALF : (h + 1) * HALF], banks[t, h][:, :HALF], COPY, scale=scale[:, t : t + 1])
+        y, v, w = rows("y", S), rows("v", 2 * S), rows("w", 2 * S)
+        y_m2, v_s = [tile[:, S:] for tile in v], [tile[:, S:] for tile in w]
+        xw = keep.tile([P, S], U32, name="xw", tag="x_small", align_bytes=64)
+        pieces = [(0, cols) for cols in halves] + [(t, slice(0, S)) for t in range(1, PACK)]
+        banks = []
+        for t, cols in pieces:
+            if t == 0:
+                nc.vector.tensor_copy(xw[:, cols], xw_raw[:].bitcast(U32).indirect(entries(offs_sb, cols)))
+            bank = psum.tile([P, S], F32, name="bank_y%d_%d" % (t, cols.start), tag="bank")
+            product(bank[:, cols], w1, w1s, t, xw[:, cols], xs[:, cols])
+            banks.append(bank)
+        for (t, cols), bank in zip(pieces, banks):
+            nc.scalar.activation(y[t][:, cols], bank[:, cols], COPY, scale=gain[:, t : t + 1])
+            for part in halves if t > 0 else [cols]:
+                nc.scalar.activation(y_m2[t][:, part], bank[:, part], COPY, scale=gain_m2[:, t : t + 1])
 
         res_sb = keep.tile([P, PACK, S], F32, name="res_sb", tag="big", align_bytes=64)
         nc.sync.dma_start(res_sb[:], res.rearrange("(p t) j -> p t j", t=PACK))
         w2 = deal_words(w2_raw, "w2", "w2")
         w2s = deal_scales(w2s_raw, "w2s", "w2s")
+        w3_raw = load_words(nc.sync, w3_words, "w3_raw")
+        load_scale_rows(nc.sync, w3s_raw, w3_scales, range(4))
 
-        def stage(window, plain, lst, name, factor):
-            dst, scaled = rows(name), rows(name + "_s")
+        def stage(window, plain, lst, parts, dst, scaled, factor):
             for t in range(PACK):
-                for h in range(2):
-                    cols = slice(h * HALF, (h + 1) * HALF)
-                    nc.vector.tensor_tensor(dst[t][:, cols], window[t][:].indirect(entries(lst, h * HALF, HALF)), plain[t][:, cols], ADD)
-                nc.scalar.activation(scaled[t][:], dst[t][:], COPY, scale=factor)
-            return dst, scaled
+                for cols in parts:
+                    nc.vector.tensor_tensor(dst[t][:, cols], window[t][:].indirect(entries(lst, cols)), plain[t][:, cols], ADD)
+                nc.scalar.activation(scaled[t], dst[t][:, :S], COPY, scale=factor)
 
-        v, v_s = stage(y, y_m2, d1_sb, "v", 0.5)
-        w, w_s = stage(v, v_s, d1_sb, "w", -4.0)
-        u, u_s = stage(w, w_s, d2_sb, "u", 0.25)
+        whole = [slice(0, S)]
+        stage(y, y_m2, d1_sb, halves, v, v_s, 0.5)
+        w_s = [tile[:] for tile in rows("w_s", S)]
+        stage(v, v_s, d1_sb, whole, w, w_s, -4.0)
+        u, u_s = rows("u", S), [tile[:] for tile in rows("u_s", S)]
+        stage(w, w_s, d2_sb, whole, u, u_s, 0.25)
 
-        gain_rows = keep.tile([P, PACK, CHUNK], F32, name="gain_rows")
-        nc.scalar.copy(gain_rows[:], gn_sb[:].unsqueeze(2).to_broadcast([P, PACK, CHUNK]))
+        gain_rows = keep.tile([P, PACK - SCALAR_TILES, max(OUT_CHUNKS)], F32, name="gain_rows")
+        nc.scalar.copy(gain_rows[:], gn_sb[:, : PACK - SCALAR_TILES].unsqueeze(2).to_broadcast([P, PACK - SCALAR_TILES, max(OUT_CHUNKS)]))
 
-        hid = rows("hid")
-
-        def fetch(window, lst, plain, op, c, name, tag):
-            dst = keep.tile([P, PACK, CHUNK], F32, name=name, tag=tag)
-            for t in range(PACK):
-                nc.vector.tensor_tensor(dst[:, t, :], window[t][:].indirect(entries(lst, c * CHUNK, CHUNK)), plain(t), op)
-            return dst
+        hid = rows("hid", S)
 
         def chunk_product(woven, words, scales, name):
-            codes = keep.tile([P, CHUNK], U32, name=name + "_codes", align_bytes=64)
-            code_scales = keep.tile([P, CHUNK], U8, name=name + "_scales", align_bytes=64)
+            width = woven.shape[1]
+            codes = keep.tile([P, width], U32, name=name + "_codes", align_bytes=64)
+            code_scales = keep.tile([P, width], U8, name=name + "_scales", align_bytes=64)
             quantize(woven, codes[:], code_scales[:])
-            bank = psum.tile([P, S], F32, name=name + "_bank", tag="bank")
-            for t in range(PACK):
-                product(bank[:, t * CHUNK : (t + 1) * CHUNK], words, scales, t, codes[:], code_scales[:])
-            return bank
+            per_bank = S // width
+            filled = []
+            for t0 in range(0, PACK, per_bank):
+                bank = psum.tile([P, per_bank, width], F32, name="%s_bank%d" % (name, t0), tag="bank")
+                for i in range(per_bank):
+                    product(bank[:, i, :], words, scales, t0 + i, codes[:], code_scales[:])
+                filled.append((t0, bank))
+            return filled
 
-        def hidden(woven, c):
-            bank = chunk_product(woven, w2, w2s, "z%d" % c)
-            for t in range(PACK):
-                nc.scalar.activation(hid[t][:, c * CHUNK : (c + 1) * CHUNK], bank[:, t * CHUNK : (t + 1) * CHUNK], TANH)
+        def hidden(woven, cols):
+            for t0, bank in chunk_product(woven, w2, w2s, "z%d" % cols.start):
+                for i in range(bank.shape[1]):
+                    if t0 + i < PACK - SCALAR_TILES:
+                        nc.scalar.activation(hid[t0 + i][:, cols], bank[:, i, :], TANH)
+                    else:
+                        nc.scalar.activation(hid[t0 + i][:, cols], bank[:, i, :], COPY, scale=2.0)
 
-        woven_z = {}
-        for c in range(N_CHUNKS):
-            cols = slice(c * CHUNK, (c + 1) * CHUNK)
-            z = fetch(u, d2_sb, lambda t: u_s[t][:, cols], ADD, c, "z%d" % c, "z%d" % c)
-            copy = nc.vector.tensor_copy if c == N_CHUNKS - 1 else nc.scalar.copy
-            woven_z[c] = weave(copy, z, "zb%d" % c, "zb%d" % c)
+        z_cols = chunks(Z_CHUNKS)
+        woven_z = []
+        for c, cols in enumerate(z_cols):
+            z = keep.tile([P, PACK, Z_CHUNKS[c]], F32, name="z%d" % c)
+            for t in range(PACK):
+                nc.vector.tensor_tensor(z[:, t, :], u[t][:].indirect(entries(d2_sb, cols)), u_s[t][:, cols], ADD)
+            copy = nc.vector.tensor_copy if c == len(z_cols) - 1 else nc.scalar.copy
+            woven_z.append(weave(copy, z, "zb%d" % c))
             if c > 0:
-                hidden(woven_z[c - 1], c - 1)
-        hidden(woven_z[N_CHUNKS - 1], N_CHUNKS - 1)
-        w3 = deal_words(w3_raw, "w3", "zb%d" % (N_CHUNKS - 1))
-        w3s = deal_scales(w3s_raw, "w3s", "zb%d" % (N_CHUNKS - 2))
+                hidden(woven_z[c - 1], z_cols[c - 1])
+        hidden(woven_z[-1], z_cols[-1])
+        w3 = deal_words(w3_raw, "w3", "zb%d" % (len(z_cols) - 1))
+        w3s = deal_scales(w3s_raw, "w3s", "w_raw")
 
         out_rows = out_0.rearrange("(p t) j -> p t j", t=PACK)
         out_words = out_1[0].rearrange("p n t -> p (n t)").bitcast(I32)
         out_scales = keep.tile([P, S], U8, name="out_scales", align_bytes=64)
+        out_cols = chunks(OUT_CHUNKS)
         woven_z2, banks3, woven_out = {}, {}, {}
 
+        def fetch(c):
+            cols, width = out_cols[c], OUT_CHUNKS[c]
+            z2 = keep.tile([P, PACK, width], F32, name="z2_%d" % c)
+            for t in range(PACK):
+                window = hid[t][:].indirect(entries(mv_sb, cols))
+                if t < PACK - SCALAR_TILES:
+                    nc.vector.tensor_tensor(z2[:, t, :], window, gain_rows[:, t, :width], MULT)
+                else:
+                    sig = keep.tile([P, width], F32, name="sig%d_%d" % (c, t))
+                    nc.scalar.activation(sig[:], window, SIGMOID)
+                    nc.scalar.activation(z2[:, t, :], sig[:], IDENTITY, scale=gn_twice[:, t : t + 1], bias=gn_minus[:, t : t + 1])
+            woven_z2[c] = weave(nc.scalar.copy, z2, "z2b%d" % c)
+
         def finish(c):
-            cols = slice(c * CHUNK, (c + 1) * CHUNK)
-            result = keep.tile([P, PACK, CHUNK], F32, name="result%d" % c)
-            nc.vector.tensor_tensor(result[:], banks3[c][:].rearrange("p (t n) -> p t n", t=PACK), res_sb[:, :, cols], ADD)
+            cols = out_cols[c]
+            result = keep.tile([P, PACK, OUT_CHUNKS[c]], F32, name="result%d" % c)
+            for t0, bank in banks3[c]:
+                ts = slice(t0, t0 + bank.shape[1])
+                nc.vector.tensor_tensor(result[:, ts, :], bank[:], res_sb[:, ts, cols], ADD)
             nc.sync.dma_start(out_rows[:, :, cols], result[:])
-            woven_out[c] = weave(nc.scalar.copy, result, "ob%d" % c, "ob%d" % c)
+            woven_out[c] = weave(nc.vector.tensor_copy if c == len(out_cols) - 1 else nc.scalar.copy, result, "ob%d" % c)
 
         def planes(c):
-            cols = slice(c * CHUNK, (c + 1) * CHUNK)
-            codes = keep.tile([P, CHUNK], U32, name="out_codes%d" % c, align_bytes=64)
+            cols = out_cols[c]
+            codes = keep.tile([P, OUT_CHUNKS[c]], U32, name="out_codes%d" % c, align_bytes=64)
             quantize(woven_out[c], codes[:], out_scales[:, cols])
             nc.sync.dma_start(out_words[:, cols], codes[:].bitcast(I32))
 
-        for step in range(N_CHUNKS + 3):
-            if step < N_CHUNKS:
-                z2 = fetch(hid, mv_sb, lambda t: gain_rows[:, t, :], MULT, step, "z2_%d" % step, "z2_%d" % step)
-                woven_z2[step] = weave(nc.scalar.copy, z2, "z2b%d" % step, "z2b%d" % step)
-            if 0 <= step - 1 < N_CHUNKS:
+        count = len(out_cols)
+        for step in range(count + 3):
+            if step < count:
+                fetch(step)
+            if 0 <= step - 1 < count:
                 banks3[step - 1] = chunk_product(woven_z2[step - 1], w3, w3s, "z2q%d" % (step - 1))
-            if 0 <= step - 2 < N_CHUNKS:
+            if 0 <= step - 2 < count:
                 finish(step - 2)
-            if 0 <= step - 3 < N_CHUNKS:
+            if 0 <= step - 3 < count:
                 planes(step - 3)
         for q in range(4):
             queue = nc.sync if q % 2 == 0 else nc.scalar

@@ -22,8 +22,8 @@ PACK = 4
 T = 2048
 S = 512
 HALF = 256
-Z_CHUNKS = [128, 128, 128, 128]
-OUT_CHUNKS = [128, 128, 128, 128]
+Z_CHUNKS = [256, 128, 128]
+OUT_CHUNKS = [256, 128, 128]
 SCALAR_TILES = 1
 FLOPS = 3 * 2 * 512 * 512 * 512
 
@@ -47,8 +47,8 @@ def tile_picked_allpass2_none_po_kernel(tc, x_words, x_scales, w1_words, w1_scal
             for q in quadrants:
                 queue.dma_start(tile[32 * q : 32 * q + 4, :].bitcast(I32), src[0, 4 * q : 4 * q + 4, :].bitcast(I32))
 
-        def load_words(queue, src, name):
-            raw = keep.tile([P, 2 * S], U8, name=name, tag="w_raw", align_bytes=64)
+        def load_words(queue, src, name, tag):
+            raw = keep.tile([P, 2 * S], U8, name=name, tag=tag, align_bytes=64)
             queue.dma_start(raw[:].bitcast(I32), src[0].bitcast(I32))
             return raw
 
@@ -90,8 +90,8 @@ def tile_picked_allpass2_none_po_kernel(tc, x_words, x_scales, w1_words, w1_scal
         def weave(copy, src, name):
             woven = keep.tile([P, src.shape[2], PACK], BF16, name=name, align_bytes=64)
             copy(
-                woven[:].rearrange("p (c i) t -> p c t i", i=4),
-                src[:].rearrange("p t (c i) -> p c t i", i=4),
+                woven[:],
+                src[:].rearrange("p t c -> p c t"),
             )
             return woven
 
@@ -103,19 +103,20 @@ def tile_picked_allpass2_none_po_kernel(tc, x_words, x_scales, w1_words, w1_scal
 
         halves = chunks([HALF, HALF])
 
-        xs_raw = keep.tile([P, T], U8, name="xs_raw", tag="x_small", align_bytes=64)
+        xs_raw = keep.tile([P, T], U8, name="xs_raw", align_bytes=64)
         nc.vector.memset(xs_raw[:, : T // 2].bitcast(I32), 0)
         nc.gpsimd.memset(xs_raw[:, T // 2 :].bitcast(I32), 0)
         w1s_raw = zeroed_scales("w1s_raw", S)
-        w1_raw = load_words(nc.sync, w1_words, "w1_raw")
-        load_scale_rows(nc.sync, xs_raw, x_scales, range(4))
-        gn_sb = keep.tile([P, PACK], F32, name="gn_sb")
-        nc.scalar.dma_start(gn_sb[:], gn.rearrange("(p t) o -> p (t o)", t=PACK))
+        w1_raw = load_words(nc.sync, w1_words, "w1_raw", "w1_raw")
+        w2_raw = load_words(nc.scalar, w2_words, "w2_raw", "w_raw")
+        load_scale_rows(nc.sync, xs_raw, x_scales, (0, 1))
+        load_scale_rows(nc.scalar, xs_raw, x_scales, (2, 3))
+        offs_sb = load_list(offs, "offs_sb")
         xw_raw = keep.tile([P, T], I32, name="xw_raw", tag="big", align_bytes=64)
         nc.scalar.dma_start(xw_raw[:], x_words[0].rearrange("p n t -> p (n t)").bitcast(I32))
-        offs_sb = load_list(offs, "offs_sb")
-        load_scale_rows(nc.sync, w1s_raw, w1_scales, (0, 1))
-        load_scale_rows(nc.gpsimd, w1s_raw, w1_scales, (2, 3))
+        load_scale_rows(nc.sync, w1s_raw, w1_scales, range(4))
+        gn_sb = keep.tile([P, PACK], F32, name="gn_sb")
+        nc.sync.dma_start(gn_sb[:], gn.rearrange("(p t) o -> p (t o)", t=PACK))
         d1_sb = load_list(d1, "d1_sb")
         d2_sb = load_list(d2, "d2_sb")
         mv_sb = load_list(mv, "mv_sb")
@@ -134,7 +135,6 @@ def tile_picked_allpass2_none_po_kernel(tc, x_words, x_scales, w1_words, w1_scal
         nc.scalar.activation(gn_minus[:], gn_sb[:], COPY, scale=-1.0)
 
         w1 = deal_words(w1_raw, "w1", "w1")
-        w2_raw = load_words(nc.sync, w2_words, "w2_raw")
         load_scale_rows(nc.sync, w2s_raw, w2_scales, range(4))
         xs = keep.tile([P, S], U8, name="xs", align_bytes=64)
         nc.vector.tensor_copy(xs[:], xs_raw[:].indirect(offs_sb[:]))
@@ -142,7 +142,7 @@ def tile_picked_allpass2_none_po_kernel(tc, x_words, x_scales, w1_words, w1_scal
 
         y, v, w = rows("y", S), rows("v", 2 * S), rows("w", 2 * S)
         y_m2, v_s = [tile[:, S:] for tile in v], [tile[:, S:] for tile in w]
-        xw = keep.tile([P, S], U32, name="xw", tag="x_small", align_bytes=64)
+        xw = keep.tile([P, S], U32, name="xw", align_bytes=64)
         pieces = [(0, cols) for cols in halves] + [(t, slice(0, S)) for t in range(1, PACK)]
         banks = []
         for t, cols in pieces:
@@ -160,7 +160,7 @@ def tile_picked_allpass2_none_po_kernel(tc, x_words, x_scales, w1_words, w1_scal
         nc.sync.dma_start(res_sb[:], res.rearrange("(p t) j -> p t j", t=PACK))
         w2 = deal_words(w2_raw, "w2", "w2")
         w2s = deal_scales(w2s_raw, "w2s", "w2s")
-        w3_raw = load_words(nc.sync, w3_words, "w3_raw")
+        w3_raw = load_words(nc.sync, w3_words, "w3_raw", "w_raw")
         load_scale_rows(nc.sync, w3s_raw, w3_scales, range(4))
 
         def stage(window, plain, lst, parts, dst, scaled, factor):
@@ -181,12 +181,11 @@ def tile_picked_allpass2_none_po_kernel(tc, x_words, x_scales, w1_words, w1_scal
 
         hid = rows("hid", S)
 
-        def chunk_product(woven, words, scales, name):
+        def chunk_product(woven, words, scales, name, per_bank):
             width = woven.shape[1]
             codes = keep.tile([P, width], U32, name=name + "_codes", align_bytes=64)
             code_scales = keep.tile([P, width], U8, name=name + "_scales", align_bytes=64)
             quantize(woven, codes[:], code_scales[:])
-            per_bank = S // width
             filled = []
             for t0 in range(0, PACK, per_bank):
                 bank = psum.tile([P, per_bank, width], F32, name="%s_bank%d" % (name, t0), tag="bank")
@@ -196,7 +195,7 @@ def tile_picked_allpass2_none_po_kernel(tc, x_words, x_scales, w1_words, w1_scal
             return filled
 
         def hidden(woven, cols):
-            for t0, bank in chunk_product(woven, w2, w2s, "z%d" % cols.start):
+            for t0, bank in chunk_product(woven, w2, w2s, "z%d" % cols.start, 1):
                 for i in range(bank.shape[1]):
                     if t0 + i < PACK - SCALAR_TILES:
                         nc.scalar.activation(hid[t0 + i][:, cols], bank[:, i, :], TANH)
@@ -206,7 +205,7 @@ def tile_picked_allpass2_none_po_kernel(tc, x_words, x_scales, w1_words, w1_scal
         z_cols = chunks(Z_CHUNKS)
         woven_z = []
         for c, cols in enumerate(z_cols):
-            z = keep.tile([P, PACK, Z_CHUNKS[c]], F32, name="z%d" % c)
+            z = keep.tile([P, PACK, Z_CHUNKS[c]], F32, name="z%d" % c, tag="zb%d" % (c - 2), align_bytes=64)
             for t in range(PACK):
                 nc.vector.tensor_tensor(z[:, t, :], u[t][:].indirect(entries(d2_sb, cols)), u_s[t][:, cols], ADD)
             copy = nc.vector.tensor_copy if c == len(z_cols) - 1 else nc.scalar.copy
@@ -256,7 +255,7 @@ def tile_picked_allpass2_none_po_kernel(tc, x_words, x_scales, w1_words, w1_scal
             if step < count:
                 fetch(step)
             if 0 <= step - 1 < count:
-                banks3[step - 1] = chunk_product(woven_z2[step - 1], w3, w3s, "z2q%d" % (step - 1))
+                banks3[step - 1] = chunk_product(woven_z2[step - 1], w3, w3s, "z2q%d" % (step - 1), S // OUT_CHUNKS[step - 1])
             if 0 <= step - 2 < count:
                 finish(step - 2)
             if 0 <= step - 3 < count:

@@ -22,7 +22,7 @@ PACK = 4
 T = 2048
 S = 512
 HALF = 256
-Z_CHUNKS = [256, 128, 128]
+Z_CHUNKS = [128, 128, 128, 128]
 OUT_CHUNKS = [256, 128, 128]
 SCALAR_TILES = 1
 FLOPS = 3 * 2 * 512 * 512 * 512
@@ -85,18 +85,17 @@ def tile_picked_allpass2_none_po_kernel(tc, x_words, x_scales, w1_words, w1_scal
             )
 
         def rows(name, width):
-            return [keep.tile([P, width], F32, name="%s_rows%d" % (name, t)) for t in range(PACK)]
+            return [keep.tile([P, width], F32, name="%s_rows%d" % (name, t), align_bytes=64) for t in range(PACK)]
 
-        def weave(copy, src, name):
+        def weave(copy, src, name, parts):
             woven = keep.tile([P, src.shape[2], PACK], BF16, name=name, align_bytes=64)
-            copy(
-                woven[:],
-                src[:].rearrange("p t c -> p c t"),
-            )
-            return woven
+            for cols in parts:
+                copy(woven[:, cols, :], src[:, :, cols].rearrange("p t c -> p c t"))
+            return woven, parts
 
         def quantize(woven, codes, scales):
-            nc.vector.quantize_mx(out=codes.bitcast(FP8X4), scales=scales, in_=woven[:].rearrange("p c t -> p (c t)"))
+            for cols in woven[1]:
+                nc.vector.quantize_mx(out=codes[:, cols].bitcast(FP8X4), scales=scales[:, cols], in_=woven[0][:, cols, :].rearrange("p c t -> p (c t)"))
 
         def chunks(widths):
             return [slice(sum(widths[:c]), sum(widths[: c + 1])) for c in range(len(widths))]
@@ -123,8 +122,6 @@ def tile_picked_allpass2_none_po_kernel(tc, x_words, x_scales, w1_words, w1_scal
         w2s_raw = zeroed_scales("w2s_raw", S)
         w3s_raw = zeroed_scales("w3s_raw", S)
 
-        warm = keep.tile([P, 1], F32, name="warm")
-        nc.scalar.activation(warm[:], gn_sb[:, 0:1], SIGMOID)
         gain = keep.tile([P, PACK], F32, name="gain")
         nc.scalar.activation(gain[:], gn_sb[:], COPY, scale=0.125)
         gain_m2 = keep.tile([P, PACK], F32, name="gain_m2")
@@ -142,24 +139,27 @@ def tile_picked_allpass2_none_po_kernel(tc, x_words, x_scales, w1_words, w1_scal
 
         y, v, w = rows("y", S), rows("v", 2 * S), rows("w", 2 * S)
         y_m2, v_s = [tile[:, S:] for tile in v], [tile[:, S:] for tile in w]
-        xw = keep.tile([P, S], U32, name="xw", align_bytes=64)
-        pieces = [(0, cols) for cols in halves] + [(t, slice(0, S)) for t in range(1, PACK)]
-        banks = []
-        for t, cols in pieces:
-            if t == 0:
-                nc.vector.tensor_copy(xw[:, cols], xw_raw[:].bitcast(U32).indirect(entries(offs_sb, cols)))
-            bank = psum.tile([P, S], F32, name="bank_y%d_%d" % (t, cols.start), tag="bank")
-            product(bank[:, cols], w1, w1s, t, xw[:, cols], xs[:, cols])
-            banks.append(bank)
-        for (t, cols), bank in zip(pieces, banks):
-            nc.scalar.activation(y[t][:, cols], bank[:, cols], COPY, scale=gain[:, t : t + 1])
-            for part in halves if t > 0 else [cols]:
-                nc.scalar.activation(y_m2[t][:, part], bank[:, part], COPY, scale=gain_m2[:, t : t + 1])
+        picked = []
+        for h, cols in enumerate(halves):
+            xw = keep.tile([P, HALF], U32, name="xw%d" % h, tag=("xw0", "w1s_raw")[h], align_bytes=64)
+            nc.vector.tensor_copy(xw[:], xw_raw[:].bitcast(U32).indirect(entries(offs_sb, cols)))
+            picked.append(xw)
+        for t in range(PACK):
+            for h, cols in enumerate(halves):
+                if t == 0 or h == 0:
+                    bank = psum.tile([P, S], F32, name="bank_y%d_%d" % (t, h), tag="bank")
+                product(bank[:, cols], w1, w1s, t, picked[h][:], xs[:, cols])
+                if t == 0:
+                    nc.scalar.activation(y[t][:, cols], bank[:, cols], COPY, scale=gain[:, t : t + 1])
+                    nc.scalar.activation(y_m2[t][:, cols], bank[:, cols], COPY, scale=gain_m2[:, t : t + 1])
+            if t > 0:
+                nc.scalar.activation(y[t][:], bank[:], COPY, scale=gain[:, t : t + 1])
+                for cols in halves:
+                    nc.scalar.activation(y_m2[t][:, cols], bank[:, cols], COPY, scale=gain_m2[:, t : t + 1])
 
         res_sb = keep.tile([P, PACK, S], F32, name="res_sb", tag="big", align_bytes=64)
         nc.sync.dma_start(res_sb[:], res.rearrange("(p t) j -> p t j", t=PACK))
         w2 = deal_words(w2_raw, "w2", "w2")
-        w2s = deal_scales(w2s_raw, "w2s", "w2s")
         w3_raw = load_words(nc.sync, w3_words, "w3_raw", "w_raw")
         load_scale_rows(nc.sync, w3s_raw, w3_scales, range(4))
 
@@ -171,18 +171,19 @@ def tile_picked_allpass2_none_po_kernel(tc, x_words, x_scales, w1_words, w1_scal
 
         whole = [slice(0, S)]
         stage(y, y_m2, d1_sb, halves, v, v_s, 0.5)
+        w2s = deal_scales(w2s_raw, "w2s", "y_rows3")
         w_s = [tile[:] for tile in rows("w_s", S)]
         stage(v, v_s, d1_sb, whole, w, w_s, -4.0)
         u, u_s = rows("u", S), [tile[:] for tile in rows("u_s", S)]
         stage(w, w_s, d2_sb, whole, u, u_s, 0.25)
 
-        gain_rows = keep.tile([P, PACK - SCALAR_TILES, max(OUT_CHUNKS)], F32, name="gain_rows")
+        gain_rows = keep.tile([P, PACK - SCALAR_TILES, max(OUT_CHUNKS)], F32, name="gain_rows", tag="y_rows0", align_bytes=64)
         nc.scalar.copy(gain_rows[:], gn_sb[:, : PACK - SCALAR_TILES].unsqueeze(2).to_broadcast([P, PACK - SCALAR_TILES, max(OUT_CHUNKS)]))
 
         hid = rows("hid", S)
 
         def chunk_product(woven, words, scales, name, per_bank):
-            width = woven.shape[1]
+            width = woven[0].shape[1]
             codes = keep.tile([P, width], U32, name=name + "_codes", align_bytes=64)
             code_scales = keep.tile([P, width], U8, name=name + "_scales", align_bytes=64)
             quantize(woven, codes[:], code_scales[:])
@@ -209,7 +210,7 @@ def tile_picked_allpass2_none_po_kernel(tc, x_words, x_scales, w1_words, w1_scal
             for t in range(PACK):
                 nc.vector.tensor_tensor(z[:, t, :], u[t][:].indirect(entries(d2_sb, cols)), u_s[t][:, cols], ADD)
             copy = nc.vector.tensor_copy if c == len(z_cols) - 1 else nc.scalar.copy
-            woven_z.append(weave(copy, z, "zb%d" % c))
+            woven_z.append(weave(copy, z, "zb%d" % c, chunks([64, 64] if c == len(z_cols) - 1 else [Z_CHUNKS[c]])))
             if c > 0:
                 hidden(woven_z[c - 1], z_cols[c - 1])
         hidden(woven_z[-1], z_cols[-1])
@@ -233,16 +234,18 @@ def tile_picked_allpass2_none_po_kernel(tc, x_words, x_scales, w1_words, w1_scal
                     sig = keep.tile([P, width], F32, name="sig%d_%d" % (c, t))
                     nc.scalar.activation(sig[:], window, SIGMOID)
                     nc.scalar.activation(z2[:, t, :], sig[:], IDENTITY, scale=gn_twice[:, t : t + 1], bias=gn_minus[:, t : t + 1])
-            woven_z2[c] = weave(nc.scalar.copy, z2, "z2b%d" % c)
+            woven_z2[c] = weave(nc.scalar.copy, z2, "z2b%d" % c, chunks([width]))
 
         def finish(c):
             cols = out_cols[c]
             result = keep.tile([P, PACK, OUT_CHUNKS[c]], F32, name="result%d" % c)
+            parts = chunks([64, 64] if c == len(out_cols) - 1 else [OUT_CHUNKS[c]])
             for t0, bank in banks3[c]:
                 ts = slice(t0, t0 + bank.shape[1])
-                nc.vector.tensor_tensor(result[:, ts, :], bank[:], res_sb[:, ts, cols], ADD)
+                for part in parts:
+                    nc.vector.tensor_tensor(result[:, ts, part], bank[:, :, part], res_sb[:, ts, cols][:, :, part], ADD)
             nc.sync.dma_start(out_rows[:, :, cols], result[:])
-            woven_out[c] = weave(nc.vector.tensor_copy if c == len(out_cols) - 1 else nc.scalar.copy, result, "ob%d" % c)
+            woven_out[c] = weave(nc.vector.tensor_copy if c == len(out_cols) - 1 else nc.scalar.copy, result, "ob%d" % c, parts)
 
         def planes(c):
             cols = out_cols[c]

@@ -122,6 +122,8 @@ def tile_picked_allpass2_none_po_kernel(tc, x_words, x_scales, w1_words, w1_scal
         w2s_raw = zeroed_scales("w2s_raw", S)
         w3s_raw = zeroed_scales("w3s_raw", S)
 
+        warm = keep.tile([P, 1], F32, name="warm")
+        nc.scalar.activation(warm[:], gn_sb[:, 0:1], SIGMOID)
         gain = keep.tile([P, PACK], F32, name="gain")
         nc.scalar.activation(gain[:], gn_sb[:], COPY, scale=0.125)
         gain_m2 = keep.tile([P, PACK], F32, name="gain_m2")

from contextlib import ExitStack

import concourse.mybir as mybir

F32 = mybir.dt.float32
BF16 = mybir.dt.bfloat16
I32 = mybir.dt.int32
U32 = mybir.dt.uint32
U16 = mybir.dt.uint16
U8 = mybir.dt.uint8
FP8X4 = mybir.dt.float8_e4m3fn_x4
FP4X4 = mybir.dt.float4_e2m1fn_x4
ADD = mybir.AluOpType.add
MULT = mybir.AluOpType.mult
COPY = mybir.ActivationFunctionType.Copy
IDENTITY = mybir.ActivationFunctionType.Identity
SIGMOID = mybir.ActivationFunctionType.Sigmoid
TANH = mybir.ActivationFunctionType.Tanh

P = 128
PACK = 4
T = 2048
S = 512
HALF = 256
Z_CHUNKS = [128, 128, 128, 128]
OUT_CHUNKS = [256, 128, 128]
SCALAR_TILES = 1
FLOPS = 3 * 2 * 512 * 512 * 512


def tile_picked_allpass2_none_po_kernel(tc, x_words, x_scales, w1_words, w1_scales, gn, w2_words, w2_scales, res, w3_words, w3_scales, offs, d1, d2, mv, out_0, out_1, out_2):
    nc = tc.nc
    with ExitStack() as ctx:
        lists = ctx.enter_context(tc.tile_pool(name="lists", bufs=1))
        keep = ctx.enter_context(tc.tile_pool(name="keep", bufs=1))
        psum = ctx.enter_context(tc.psum_pool(name="psum", bufs=8))

        def load_list(src, name):
            tile = lists.tile([P, S // 16], U16, name=name)
            nc.sync.dma_start(tile[:], src)
            return tile

        def entries(tile, cols):
            return tile[:, cols.start // 16 : cols.stop // 16]

        def load_scale_rows(queue, tile, src, quadrants):
            for q in quadrants:
                queue.dma_start(tile[32 * q : 32 * q + 4, :].bitcast(I32), src[0, 4 * q : 4 * q + 4, :].bitcast(I32))

        def load_words(queue, src, name, tag):
            raw = keep.tile([P, 2 * S], U8, name=name, tag=tag, align_bytes=64)
            queue.dma_start(raw[:].bitcast(I32), src[0].bitcast(I32))
            return raw

        def deal_words(raw, name, tag):
            dealt = keep.tile([P, 2 * S], U8, name=name, tag=tag, align_bytes=64)
            nc.vector.tensor_copy(
                dealt[:].bitcast(U16).rearrange("p (t m) -> p t m", t=PACK),
                raw[:].bitcast(U16).rearrange("p (m t) -> p t m", t=PACK),
            )
            return dealt

        def deal_scales(raw, name, tag):
            dealt = keep.tile([P, S], U8, name=name, tag=tag, align_bytes=64)
            nc.vector.tensor_copy(
                dealt[:].rearrange("p (t m) -> p t m", t=PACK),
                raw[:].rearrange("p (m t) -> p t m", t=PACK),
            )
            return dealt

        def zeroed_scales(name, width):
            raw = keep.tile([P, width], U8, name=name, align_bytes=64)
            nc.gpsimd.memset(raw[:].bitcast(I32), 0)
            return raw

        def product(dst, words, scales, t, codes, code_scales):
            nc.tensor.matmul_mx(
                out=dst,
                lhsT=words[:, 2 * P * t : 2 * P * (t + 1)].bitcast(FP4X4),
                lhsT_scale=scales[:, P * t : P * (t + 1)],
                rhs=codes.bitcast(FP8X4),
                rhs_scale=code_scales,
                start=True,
                stop=True,
            )

        def rows(name, width):
            return [keep.tile([P, width], F32, name="%s_rows%d" % (name, t), align_bytes=64) for t in range(PACK)]

        def weave(copy, src, name, parts):
            woven = keep.tile([P, src.shape[2], PACK], BF16, name=name, align_bytes=64)
            for cols in parts:
                copy(woven[:, cols, :], src[:, :, cols].rearrange("p t c -> p c t"))
            return woven, parts

        def quantize(woven, codes, scales):
            for cols in woven[1]:
                nc.vector.quantize_mx(out=codes[:, cols].bitcast(FP8X4), scales=scales[:, cols], in_=woven[0][:, cols, :].rearrange("p c t -> p (c t)"))

        def chunks(widths):
            return [slice(sum(widths[:c]), sum(widths[: c + 1])) for c in range(len(widths))]

        halves = chunks([HALF, HALF])

        xs_raw = keep.tile([P, T], U8, name="xs_raw", align_bytes=64)
        nc.vector.memset(xs_raw[:, : T // 2].bitcast(I32), 0)
        nc.gpsimd.memset(xs_raw[:, T // 2 :].bitcast(I32), 0)
        w1s_raw = zeroed_scales("w1s_raw", S)
        w1_raw = load_words(nc.sync, w1_words, "w1_raw", "w1_raw")
        w2_raw = load_words(nc.scalar, w2_words, "w2_raw", "w_raw")
        load_scale_rows(nc.sync, xs_raw, x_scales, (0, 1))
        load_scale_rows(nc.scalar, xs_raw, x_scales, (2, 3))
        offs_sb = load_list(offs, "offs_sb")
        xw_raw = keep.tile([P, T], I32, name="xw_raw", tag="big", align_bytes=64)
        nc.scalar.dma_start(xw_raw[:], x_words[0].rearrange("p n t -> p (n t)").bitcast(I32))
        load_scale_rows(nc.sync, w1s_raw, w1_scales, range(4))
        gn_sb = keep.tile([P, PACK], F32, name="gn_sb")
        nc.sync.dma_start(gn_sb[:], gn.rearrange("(p t) o -> p (t o)", t=PACK))
        d1_sb = load_list(d1, "d1_sb")
        d2_sb = load_list(d2, "d2_sb")
        mv_sb = load_list(mv, "mv_sb")
        w2s_raw = zeroed_scales("w2s_raw", S)
        w3s_raw = zeroed_scales("w3s_raw", S)

        warm = keep.tile([P, 1], F32, name="warm")
        nc.scalar.activation(warm[:], gn_sb[:, 0:1], SIGMOID)
        gain = keep.tile([P, PACK], F32, name="gain")
        nc.scalar.activation(gain[:], gn_sb[:], COPY, scale=0.125)
        gain_m2 = keep.tile([P, PACK], F32, name="gain_m2")
        nc.scalar.activation(gain_m2[:], gn_sb[:], COPY, scale=-0.25)
        gn_twice = keep.tile([P, PACK], F32, name="gn_twice")
        nc.scalar.activation(gn_twice[:], gn_sb[:], COPY, scale=2.0)
        gn_minus = keep.tile([P, PACK], F32, name="gn_minus")
        nc.scalar.activation(gn_minus[:], gn_sb[:], COPY, scale=-1.0)

        w1 = deal_words(w1_raw, "w1", "w1")
        load_scale_rows(nc.sync, w2s_raw, w2_scales, range(4))
        xs = keep.tile([P, S], U8, name="xs", align_bytes=64)
        nc.vector.tensor_copy(xs[:], xs_raw[:].indirect(offs_sb[:]))
        w1s = deal_scales(w1s_raw, "w1s", "w1s")

        y, v, w = rows("y", S), rows("v", 2 * S), rows("w", 2 * S)
        y_m2, v_s = [tile[:, S:] for tile in v], [tile[:, S:] for tile in w]
        picked = []
        for h, cols in enumerate(halves):
            xw = keep.tile([P, HALF], U32, name="xw%d" % h, tag=("xw0", "w1s_raw")[h], align_bytes=64)
            nc.vector.tensor_copy(xw[:], xw_raw[:].bitcast(U32).indirect(entries(offs_sb, cols)))
            picked.append(xw)
        for t in range(PACK):
            for h, cols in enumerate(halves):
                if t == 0 or h == 0:
                    bank = psum.tile([P, S], F32, name="bank_y%d_%d" % (t, h), tag="bank")
                product(bank[:, cols], w1, w1s, t, picked[h][:], xs[:, cols])
                if t == 0:
                    nc.scalar.activation(y[t][:, cols], bank[:, cols], COPY, scale=gain[:, t : t + 1])
                    nc.scalar.activation(y_m2[t][:, cols], bank[:, cols], COPY, scale=gain_m2[:, t : t + 1])
            if t > 0:
                nc.scalar.activation(y[t][:], bank[:], COPY, scale=gain[:, t : t + 1])
                for cols in halves:
                    nc.scalar.activation(y_m2[t][:, cols], bank[:, cols], COPY, scale=gain_m2[:, t : t + 1])

        res_sb = keep.tile([P, PACK, S], F32, name="res_sb", tag="big", align_bytes=64)
        nc.sync.dma_start(res_sb[:], res.rearrange("(p t) j -> p t j", t=PACK))
        w2 = deal_words(w2_raw, "w2", "w2")
        w3_raw = load_words(nc.sync, w3_words, "w3_raw", "w_raw")
        load_scale_rows(nc.sync, w3s_raw, w3_scales, range(4))

        def stage(window, plain, lst, parts, dst, scaled, factor):
            for t in range(PACK):
                for cols in parts:
                    nc.vector.tensor_tensor(dst[t][:, cols], window[t][:].indirect(entries(lst, cols)), plain[t][:, cols], ADD)
                nc.scalar.activation(scaled[t], dst[t][:, :S], COPY, scale=factor)

        whole = [slice(0, S)]
        stage(y, y_m2, d1_sb, halves, v, v_s, 0.5)
        w2s = deal_scales(w2s_raw, "w2s", "y_rows3")
        w_s = [tile[:] for tile in rows("w_s", S)]
        stage(v, v_s, d1_sb, whole, w, w_s, -4.0)
        u, u_s = rows("u", S), [tile[:] for tile in rows("u_s", S)]
        stage(w, w_s, d2_sb, whole, u, u_s, 0.25)

        gain_rows = keep.tile([P, PACK - SCALAR_TILES, max(OUT_CHUNKS)], F32, name="gain_rows", tag="y_rows0", align_bytes=64)
        nc.scalar.copy(gain_rows[:], gn_sb[:, : PACK - SCALAR_TILES].unsqueeze(2).to_broadcast([P, PACK - SCALAR_TILES, max(OUT_CHUNKS)]))

        hid = rows("hid", S)

        def chunk_product(woven, words, scales, name, per_bank):
            width = woven[0].shape[1]
            codes = keep.tile([P, width], U32, name=name + "_codes", align_bytes=64)
            code_scales = keep.tile([P, width], U8, name=name + "_scales", align_bytes=64)
            quantize(woven, codes[:], code_scales[:])
            filled = []
            for t0 in range(0, PACK, per_bank):
                bank = psum.tile([P, per_bank, width], F32, name="%s_bank%d" % (name, t0), tag="bank")
                for i in range(per_bank):
                    product(bank[:, i, :], words, scales, t0 + i, codes[:], code_scales[:])
                filled.append((t0, bank))
            return filled

        def hidden(woven, cols):
            for t0, bank in chunk_product(woven, w2, w2s, "z%d" % cols.start, 1):
                for i in range(bank.shape[1]):
                    if t0 + i < PACK - SCALAR_TILES:
                        nc.scalar.activation(hid[t0 + i][:, cols], bank[:, i, :], TANH)
                    else:
                        nc.scalar.activation(hid[t0 + i][:, cols], bank[:, i, :], COPY, scale=2.0)

        z_cols = chunks(Z_CHUNKS)
        woven_z = []
        for c, cols in enumerate(z_cols):
            z = keep.tile([P, PACK, Z_CHUNKS[c]], F32, name="z%d" % c, tag="zb%d" % (c - 2), align_bytes=64)
            for t in range(PACK):
                nc.vector.tensor_tensor(z[:, t, :], u[t][:].indirect(entries(d2_sb, cols)), u_s[t][:, cols], ADD)
            copy = nc.vector.tensor_copy if c == len(z_cols) - 1 else nc.scalar.copy
            woven_z.append(weave(copy, z, "zb%d" % c, chunks([64, 64] if c == len(z_cols) - 1 else [Z_CHUNKS[c]])))
            if c > 0:
                hidden(woven_z[c - 1], z_cols[c - 1])
        hidden(woven_z[-1], z_cols[-1])
        w3 = deal_words(w3_raw, "w3", "zb%d" % (len(z_cols) - 1))
        w3s = deal_scales(w3s_raw, "w3s", "w_raw")

        out_rows = out_0.rearrange("(p t) j -> p t j", t=PACK)
        out_words = out_1[0].rearrange("p n t -> p (n t)").bitcast(I32)
        out_scales = keep.tile([P, S], U8, name="out_scales", align_bytes=64)
        out_cols = chunks(OUT_CHUNKS)
        woven_z2, banks3, woven_out = {}, {}, {}

        def fetch(c):
            cols, width = out_cols[c], OUT_CHUNKS[c]
            z2 = keep.tile([P, PACK, width], F32, name="z2_%d" % c)
            for t in range(PACK):
                window = hid[t][:].indirect(entries(mv_sb, cols))
                if t < PACK - SCALAR_TILES:
                    nc.vector.tensor_tensor(z2[:, t, :], window, gain_rows[:, t, :width], MULT)
                else:
                    sig = keep.tile([P, width], F32, name="sig%d_%d" % (c, t))
                    nc.scalar.activation(sig[:], window, SIGMOID)
                    nc.scalar.activation(z2[:, t, :], sig[:], IDENTITY, scale=gn_twice[:, t : t + 1], bias=gn_minus[:, t : t + 1])
            woven_z2[c] = weave(nc.scalar.copy, z2, "z2b%d" % c, chunks([width]))

        def finish(c):
            cols = out_cols[c]
            result = keep.tile([P, PACK, OUT_CHUNKS[c]], F32, name="result%d" % c)
            parts = chunks([64, 64] if c == len(out_cols) - 1 else [OUT_CHUNKS[c]])
            for t0, bank in banks3[c]:
                ts = slice(t0, t0 + bank.shape[1])
                for part in parts:
                    nc.vector.tensor_tensor(result[:, ts, part], bank[:, :, part], res_sb[:, ts, cols][:, :, part], ADD)
            nc.sync.dma_start(out_rows[:, :, cols], result[:])
            woven_out[c] = weave(nc.vector.tensor_copy if c == len(out_cols) - 1 else nc.scalar.copy, result, "ob%d" % c, parts)

        def planes(c):
            cols = out_cols[c]
            codes = keep.tile([P, OUT_CHUNKS[c]], U32, name="out_codes%d" % c, align_bytes=64)
            quantize(woven_out[c], codes[:], out_scales[:, cols])
            nc.sync.dma_start(out_words[:, cols], codes[:].bitcast(I32))

        count = len(out_cols)
        for step in range(count + 3):
            if step < count:
                fetch(step)
            if 0 <= step - 1 < count:
                banks3[step - 1] = chunk_product(woven_z2[step - 1], w3, w3s, "z2q%d" % (step - 1), S // OUT_CHUNKS[step - 1])
            if 0 <= step - 2 < count:
                finish(step - 2)
            if 0 <= step - 3 < count:
                planes(step - 3)
        for q in range(4):
            queue = nc.sync if q % 2 == 0 else nc.scalar
            queue.dma_start(out_2[0, 4 * q : 4 * q + 4, :].bitcast(I32), out_scales[32 * q : 32 * q + 4, :].bitcast(I32))
